import numpy as np
import ml_dtypes


def mxq(x, axis, fmt="e4m3"):
    dtype, down = {"e4m3": (ml_dtypes.float8_e4m3fn, 7), "e5m2": (ml_dtypes.float8_e5m2, 14)}[fmt]
    v = np.moveaxis(np.asarray(x, np.float32).astype(ml_dtypes.bfloat16).astype(np.float64), axis, -1)
    blocks = v.reshape(v.shape[:-1] + (-1, 32))
    amax = np.abs(blocks).max(-1, keepdims=True)
    byte = np.maximum(np.where(amax > 0, np.frexp(amax)[1] - 1 + 127, 0) - down, 1)
    scale = np.exp2(byte - 127.0)
    codes = (blocks / scale).astype(np.float32).astype(dtype).astype(np.float64)
    return np.moveaxis((codes * scale).reshape(v.shape), -1, axis)


WIDE = False


def mx_kscale(k):
    if not WIDE:
        return np.ones(k)
    levels = np.array([10, -10, 5, -5, 0])
    if k % 512:
        return np.exp2(np.random.permutation(np.resize(levels, k // 32))).repeat(32)
    a = np.empty((k // 512, 16))
    for p in range(k // 512):
        a[p, :8] = np.random.permutation(np.resize(levels, 8))
        for g in range(8):
            far = levels[np.abs(levels - a[p, g]) >= 10]
            a[p, g + 8] = far[np.random.randint(len(far))]
    return np.exp2(a.ravel()).repeat(32)


def f64(x):
    return np.asarray(x).astype(np.float64)


def striped8(idx):
    return np.asarray(idx).reshape(8, -1, 16).transpose(0, 2, 1).reshape(128, -1).astype(np.uint16)


def unstriped8(offs):
    return offs.reshape(8, 16, -1).transpose(0, 2, 1).reshape(8, -1).astype(np.int64)


def pick8(x, idx, run):
    r = np.arange(len(x))
    return x[r[:, None], idx[r % (8 * run) // run]]


E2M1 = np.array([0.0, 0.5, 1.0, 1.5, 2.0, 3.0, 4.0, 6.0, -0.0, -0.5, -1.0, -1.5, -2.0, -3.0, -4.0, -6.0])


def pack_weight(w, fmt):
    k, n = w.shape
    w = f64(np.asarray(w, np.float32).astype(ml_dtypes.bfloat16)).reshape(k // 32, 32, n)
    amax = np.abs(w).max(1)
    if fmt == "e4m3":
        byte = np.frexp(amax)[1] - 1 + 127 - 7
    else:
        mant, ex = np.frexp(amax / 6.0)
        byte = np.where(mant > 0.5, ex, ex - 1) + 127
    byte = np.clip(np.where(amax > 0, byte, 1), 1, 254)
    scaled = (w * np.exp2(127.0 - byte)[:, None, :]).reshape(k, n).astype(np.float32)
    by_word = np.ascontiguousarray(scaled.reshape(k // 512, 128, 4, n).transpose(0, 1, 3, 2))
    if fmt == "e4m3":
        words = by_word.astype(ml_dtypes.float8_e4m3fn).view(np.uint8)
    else:
        c = by_word.astype(ml_dtypes.float4_e2m1fn).view(np.uint8) & 0xF
        words = (c[..., 0::2] | (c[..., 1::2] << 4)).reshape(k // 512, 128, 2 * n)
    return np.ascontiguousarray(words), np.ascontiguousarray(byte.astype(np.uint8).reshape(k // 512, 16, n))


def unpack_weight(words, scales, fmt):
    g, _, n = scales.shape
    words = np.ascontiguousarray(words).reshape(g, 128, n, -1)
    if fmt == "e4m3":
        vals = words.view(ml_dtypes.float8_e4m3fn).astype(np.float64)
    else:
        nib = np.empty((g, 128, n, 4), np.uint8)
        nib[..., 0::2] = words & 0xF
        nib[..., 1::2] = words >> 4
        vals = E2M1[nib]
    vals = vals * np.repeat(np.exp2(scales.astype(np.float64) - 127.0), 8, axis=1)[..., None]
    return vals.transpose(0, 1, 3, 2).reshape(g * 512, n)


D, T, I, Q = 512, 1024, 512, 128


def setup_inputs():
    n = np.random.standard_normal
    idx = np.stack([np.random.permutation(T)[:I] for _ in range(8)])
    idx2 = np.stack([np.random.permutation(T)[:I] for _ in range(8)])
    idx3 = np.stack([np.random.permutation(T)[:I] for _ in range(8)])
    idx4 = np.stack([np.random.permutation(T)[:I] for _ in range(8)])
    fd = mx_kscale(D)
    keysp = pack_weight(n((D, T)) / fd[:, None], "e2m1")
    return {
        "query": (n((D, Q)) * 1.0 / np.sqrt(D) * fd[:, None]).astype(np.float32),
        "keys_words": keysp[0],
        "keys_scales": keysp[1],
        "lam": (np.random.uniform(0.4, 1.0, (Q, 1))).astype(np.float32),
        "old": (1.0 * n((Q, T))).astype(np.float32),
        "share2": (np.random.uniform(0.4, 1.2, (Q, 1))).astype(np.float32),
        "offs": striped8(idx),
        "offs2": striped8(idx2),
        "offs3": striped8(idx3),
        "offs4": striped8(idx4),
    }


def reference(query, keys_words, keys_scales, lam, old, share2, offs, offs2, offs3, offs4):
    idx = unstriped8(offs)
    idx2 = unstriped8(offs2)
    idx3 = unstriped8(offs3)
    idx4 = unstriped8(offs4)
    keysu = unpack_weight(keys_words, keys_scales, "e2m1")
    queryq = mxq(f64(query), 0, "e4m3")
    a = queryq.T @ keysu
    w = pick8(a, idx, 16) + np.tanh(pick8(a, idx2, 16) - pick8(a, idx3, 16)) * f64(lam)
    f1 = np.zeros((Q, T))
    f1[np.arange(Q)[:, None], idx[np.arange(Q) % 128 // 16]] = w
    f2 = np.zeros((Q, T))
    f2[np.arange(Q)[:, None], idx4[np.arange(Q) % 128 // 16]] = w
    y = f64(old) + f1 + f2 * f64(share2)
    return y

@@ -1,0 +1,170 @@
+from contextlib import ExitStack
+
+import concourse.mybir as mybir
+from concourse.masks import make_identity
+
+D, T, SLOTS, Q = 512, 1024, 512, 128
+FLOPS = 2 * D * T * Q
+
+F32 = mybir.dt.float32
+BF16 = mybir.dt.bfloat16
+I32 = mybir.dt.int32
+U32 = mybir.dt.uint32
+U16 = mybir.dt.uint16
+U8 = mybir.dt.uint8
+FP8X4 = mybir.dt.float8_e4m3fn_x4
+FP4X4 = mybir.dt.float4_e2m1fn_x4
+ALU = mybir.AluOpType
+ACT = mybir.ActivationFunctionType
+
+P = 128
+PACK = 4
+N_MM = 256
+HALF = SLOTS // 2
+BANK = 512
+OUT_PIECES = (256, 256, 256, 128, 128)
+
+
+def tile_attend_seconded_lean_twiceput_heads_kernel(
+    tc, query, keys_words, keys_scales, lam, old, share2, offs, offs2, offs3, offs4, out
+):
+    nc = tc.nc
+    with ExitStack() as ctx:
+        lists = ctx.enter_context(tc.tile_pool(name="lists", bufs=1))
+        sb = ctx.enter_context(tc.tile_pool(name="sb", bufs=1))
+        ps = ctx.enter_context(tc.psum_pool(name="ps", bufs=1))
+
+        q_raw = sb.tile([P, PACK, Q], F32, name="q_raw")
+        nc.sync.dma_start(out=q_raw[:], in_=query.rearrange("(p j) q -> p j q", j=PACK))
+        k_words = sb.tile([P, 2 * T], U8, name="k_words", align_bytes=64)
+        nc.sync.dma_start(out=k_words[:].bitcast(I32), in_=keys_words[0].bitcast(I32))
+        k_scales = sb.tile([P, T], U8, name="k_scales", align_bytes=64)
+        nc.vector.memset(k_scales[:].bitcast(U32), 0)
+        for quad in range(4):
+            nc.scalar.dma_start(
+                out=k_scales[32 * quad : 32 * quad + 4, :].bitcast(I32),
+                in_=keys_scales[0, 4 * quad : 4 * quad + 4, :].bitcast(I32),
+            )
+
+        def load_list(src, name):
+            tile = lists.tile([P, SLOTS // 16], U16, name=name)
+            nc.sync.dma_start(tile[:], src)
+            return tile
+
+        opp_list = load_list(offs3, "opp_list")
+        own_list = load_list(offs, "own_list")
+        sec_list = load_list(offs2, "sec_list")
+        lam_col = sb.tile([P, 1], F32, name="lam_col")
+        nc.gpsimd.dma_start(out=lam_col[:], in_=lam)
+        share_col = sb.tile([P, 1], F32, name="share_col")
+        nc.gpsimd.dma_start(out=share_col[:], in_=share2)
+        old_sb = sb.tile([P, T], F32, name="old_sb")
+        nc.sync.dma_start(out=old_sb[:], in_=old)
+        put_list = load_list(offs4, "put_list")
+
+        ident = sb.tile([P, P], F32, name="ident")
+        make_identity(nc, ident[:])
+        f1 = sb.tile([P, T], F32, name="f1")
+        f2 = sb.tile([P, T], F32, name="f2")
+        nc.vector.memset(f1[:], 0.0)
+        nc.vector.memset(f2[:], 0.0)
+
+        q_bf = sb.tile([P, Q, PACK], BF16, name="q_bf", align_bytes=64)
+        nc.vector.tensor_copy(
+            out=q_bf[:].rearrange("p (c i) t -> p c t i", i=4),
+            in_=q_raw[:].rearrange("p t (c i) -> p c t i", i=4),
+        )
+        q_codes = sb.tile([P, Q], U32, name="q_codes", align_bytes=64)
+        q_scales = sb.tile([P, Q], U8, name="q_scales", align_bytes=64)
+        nc.vector.quantize_mx(
+            out=q_codes[:].bitcast(FP8X4), scales=q_scales[:], in_=q_bf[:].rearrange("p q t -> p (q t)")
+        )
+
+        a = sb.tile([P, T], F32, name="a")
+        for n in range(T // N_MM):
+            cols = slice(n * N_MM, (n + 1) * N_MM)
+            acc = ps.tile([P, N_MM], F32, name="acc%d" % n)
+            nc.tensor.matmul_mx(
+                out=acc[:],
+                lhsT=q_codes[:].bitcast(FP8X4),
+                lhsT_scale=q_scales[:],
+                rhs=k_words[:, 2 * cols.start : 2 * cols.stop].bitcast(FP4X4),
+                rhs_scale=k_scales[:, cols],
+                start=True,
+                stop=True,
+            )
+            if n % 2 == 0:
+                nc.scalar.copy(out=a[:, cols], in_=acc[:])
+            else:
+                nc.vector.tensor_copy(out=a[:, cols], in_=acc[:])
+
+        def half_of(tile, h):
+            return tile[:, h * HALF // 16 : (h + 1) * HALF // 16]
+
+        def halves(name):
+            return [sb.tile([P, HALF], F32, name="%s%d" % (name, h)) for h in range(2)]
+
+        opp, diff, lean = (halves(s) for s in ("opp", "diff", "lean"))
+        own_all = sb.tile([P, SLOTS], F32, name="own_all")
+        bonus_all = sb.tile([P, SLOTS], F32, name="bonus_all")
+        own = [own_all[:, h * HALF : (h + 1) * HALF] for h in range(2)]
+        bonus = [bonus_all[:, h * HALF : (h + 1) * HALF] for h in range(2)]
+        nc.scalar.activation(opp[0][:], a[:].indirect(half_of(opp_list, 0)), ACT.Copy)
+        nc.vector.tensor_copy(own[0], a[:].indirect(half_of(own_list, 0)))
+        nc.scalar.activation(opp[1][:], a[:].indirect(half_of(opp_list, 1)), ACT.Copy)
+        for h in range(2):
+            nc.vector.tensor_tensor(diff[h][:], a[:].indirect(half_of(sec_list, h)), opp[h][:], ALU.subtract)
+        for h in range(2):
+            nc.scalar.activation(lean[h][:], diff[h][:], ACT.Tanh)
+            nc.scalar.activation(bonus[h], lean[h][:], ACT.Copy, scale=lam_col[:])
+        nc.scalar.activation(own[1], a[:].indirect(half_of(own_list, 1)), ACT.Copy)
+        for h in range(2):
+            nc.vector.tensor_tensor(f1[:].indirect(half_of(own_list, h)), own[h], bonus[h], ALU.add)
+        nc.vector.tensor_tensor(f2[:].indirect(put_list[:]), own_all[:], bonus_all[:], ALU.add)
+
+        blocks = BANK // P
+        turned = [ps.tile([P, BANK], F32, name="turned%d" % b) for b in range(T // BANK)]
+        for b in range(T // BANK):
+            for j in range(blocks):
+                nc.tensor.matmul(
+                    turned[b][:, j * P : (j + 1) * P],
+                    old_sb[:, b * BANK + j * P : b * BANK + (j + 1) * P],
+                    ident[:],
+                    start=(j == 0),
+                    stop=False,
+                    is_transpose=True,
+                )
+        base = []
+        for b in range(T // BANK):
+            for j in range(blocks):
+                nc.tensor.matmul(
+                    turned[b][:, j * P : (j + 1) * P],
+                    f1[:, b * BANK + j * P : b * BANK + (j + 1) * P],
+                    ident[:],
+                    start=False,
+                    stop=(j == blocks - 1),
+                    is_transpose=True,
+                )
+        for b in range(T // BANK):
+            turned_sb = sb.tile([P, BANK], F32, name="turned_sb%d" % b)
+            nc.scalar.copy(out=turned_sb[:], in_=turned[b][:])
+            back = ps.tile([P, BANK], F32, name="back%d" % b)
+            for j in range(blocks):
+                nc.tensor.transpose(back[:, j * P : (j + 1) * P], turned_sb[:, j * P : (j + 1) * P], ident[:])
+            base.append(back)
+
+        start = 0
+        for i, width in enumerate(OUT_PIECES):
+            piece = sb.tile([P, width], F32, name="piece%d" % i)
+            b, off = divmod(start, BANK)
+            nc.vector.scalar_tensor_tensor(
+                out=piece[:],
+                in0=f2[:, start : start + width],
+                scalar=share_col[:],
+                in1=base[b][:, off : off + width],
+                op0=ALU.mult,
+                op1=ALU.add,
+            )
+            queue = nc.sync if i % 2 == 0 else nc.scalar
+            queue.dma_start(out=out[:, start : start + width], in_=piece[:])
+            start = start + width

@@ -19,7 +19,7 @@ ACT = mybir.ActivationFunctionType
 
 P = 128
 PACK = 4
-N_MM = 256
+MM_PIECES = (256, 256, 256, 128, 128)
 HALF = SLOTS // 2
 BANK = 512
 OUT_PIECES = (256, 256, 256, 128, 128)
@@ -34,14 +34,14 @@ def tile_attend_seconded_lean_twiceput_heads_kernel(
         sb = ctx.enter_context(tc.tile_pool(name="sb", bufs=1))
         ps = ctx.enter_context(tc.psum_pool(name="ps", bufs=1))
 
-        q_raw = sb.tile([P, PACK, Q], F32, name="q_raw")
+        q_raw = sb.tile([P, PACK, Q], F32, name="q_raw", tag="load")
         nc.sync.dma_start(out=q_raw[:], in_=query.rearrange("(p j) q -> p j q", j=PACK))
         k_words = sb.tile([P, 2 * T], U8, name="k_words", align_bytes=64)
         nc.sync.dma_start(out=k_words[:].bitcast(I32), in_=keys_words[0].bitcast(I32))
         k_scales = sb.tile([P, T], U8, name="k_scales", align_bytes=64)
         nc.vector.memset(k_scales[:].bitcast(U32), 0)
         for quad in range(4):
-            nc.scalar.dma_start(
+            nc.sync.dma_start(
                 out=k_scales[32 * quad : 32 * quad + 4, :].bitcast(I32),
                 in_=keys_scales[0, 4 * quad : 4 * quad + 4, :].bitcast(I32),
             )
@@ -52,38 +52,39 @@ def tile_attend_seconded_lean_twiceput_heads_kernel(
             return tile
 
         opp_list = load_list(offs3, "opp_list")
-        own_list = load_list(offs, "own_list")
         sec_list = load_list(offs2, "sec_list")
+        own_list = load_list(offs, "own_list")
         lam_col = sb.tile([P, 1], F32, name="lam_col")
         nc.gpsimd.dma_start(out=lam_col[:], in_=lam)
         share_col = sb.tile([P, 1], F32, name="share_col")
         nc.gpsimd.dma_start(out=share_col[:], in_=share2)
-        old_sb = sb.tile([P, T], F32, name="old_sb")
-        nc.sync.dma_start(out=old_sb[:], in_=old)
         put_list = load_list(offs4, "put_list")
 
         ident = sb.tile([P, P], F32, name="ident")
         make_identity(nc, ident[:])
-        f1 = sb.tile([P, T], F32, name="f1")
-        f2 = sb.tile([P, T], F32, name="f2")
-        nc.vector.memset(f1[:], 0.0)
-        nc.vector.memset(f2[:], 0.0)
+        f1a = sb.tile([P, T], F32, name="f1a")
+        nc.vector.memset(f1a[:], 0.0)
 
-        q_bf = sb.tile([P, Q, PACK], BF16, name="q_bf", align_bytes=64)
+        q_bf = sb.tile([P, Q, PACK], BF16, name="q_bf", tag="first", align_bytes=64)
         nc.vector.tensor_copy(
             out=q_bf[:].rearrange("p (c i) t -> p c t i", i=4),
             in_=q_raw[:].rearrange("p t (c i) -> p c t i", i=4),
         )
+        old_sb = sb.tile([P, T], F32, name="old_sb", tag="load")
+        nc.sync.dma_start(out=old_sb[:], in_=old)
         q_codes = sb.tile([P, Q], U32, name="q_codes", align_bytes=64)
         q_scales = sb.tile([P, Q], U8, name="q_scales", align_bytes=64)
         nc.vector.quantize_mx(
             out=q_codes[:].bitcast(FP8X4), scales=q_scales[:], in_=q_bf[:].rearrange("p q t -> p (q t)")
         )
 
-        a = sb.tile([P, T], F32, name="a")
-        for n in range(T // N_MM):
-            cols = slice(n * N_MM, (n + 1) * N_MM)
-            acc = ps.tile([P, N_MM], F32, name="acc%d" % n)
+        f1b = sb.tile([P, T], F32, name="f1b", tag="first", align_bytes=64)
+        nc.gpsimd.memset(f1b[:], 0.0)
+        f1 = [f1a, f1b]
+        a = sb.tile([P, T], F32, name="a", tag="row")
+        for n, width in enumerate(MM_PIECES):
+            cols = slice(sum(MM_PIECES[:n]), sum(MM_PIECES[: n + 1]))
+            acc = ps.tile([P, width], F32, name="acc%d" % n, tag="bank%d" % n)
             nc.tensor.matmul_mx(
                 out=acc[:],
                 lhsT=q_codes[:].bitcast(FP8X4),
@@ -93,7 +94,7 @@ def tile_attend_seconded_lean_twiceput_heads_kernel(
                 start=True,
                 stop=True,
             )
-            if n % 2 == 0:
+            if n % 2 == 1:
                 nc.scalar.copy(out=a[:, cols], in_=acc[:])
             else:
                 nc.vector.tensor_copy(out=a[:, cols], in_=acc[:])
@@ -104,51 +105,49 @@ def tile_attend_seconded_lean_twiceput_heads_kernel(
         def halves(name):
             return [sb.tile([P, HALF], F32, name="%s%d" % (name, h)) for h in range(2)]
 
-        opp, diff, lean = (halves(s) for s in ("opp", "diff", "lean"))
-        own_all = sb.tile([P, SLOTS], F32, name="own_all")
+        opp, diff = halves("opp"), halves("diff")
+        strip = sb.tile([P, 3 * HALF], F32, name="strip")
+        own_all = strip[:, 0:SLOTS]
         bonus_all = sb.tile([P, SLOTS], F32, name="bonus_all")
         own = [own_all[:, h * HALF : (h + 1) * HALF] for h in range(2)]
         bonus = [bonus_all[:, h * HALF : (h + 1) * HALF] for h in range(2)]
+        lean = [strip[:, 3 * HALF // 2 : 5 * HALF // 2], strip[:, 2 * HALF : 3 * HALF]]
+        sec0 = own[0]
         nc.scalar.activation(opp[0][:], a[:].indirect(half_of(opp_list, 0)), ACT.Copy)
-        nc.vector.tensor_copy(own[0], a[:].indirect(half_of(own_list, 0)))
+        nc.vector.tensor_copy(sec0, a[:].indirect(half_of(sec_list, 0)))
         nc.scalar.activation(opp[1][:], a[:].indirect(half_of(opp_list, 1)), ACT.Copy)
+        nc.vector.tensor_tensor(diff[0][:], sec0, opp[0][:], ALU.subtract)
+        nc.vector.tensor_copy(own[0], a[:].indirect(half_of(own_list, 0)))
+        nc.vector.tensor_tensor(diff[1][:], a[:].indirect(half_of(sec_list, 1)), opp[1][:], ALU.subtract)
         for h in range(2):
-            nc.vector.tensor_tensor(diff[h][:], a[:].indirect(half_of(sec_list, h)), opp[h][:], ALU.subtract)
-        for h in range(2):
-            nc.scalar.activation(lean[h][:], diff[h][:], ACT.Tanh)
-            nc.scalar.activation(bonus[h], lean[h][:], ACT.Copy, scale=lam_col[:])
+            nc.scalar.activation(lean[h], diff[h][:], ACT.Tanh)
+            nc.scalar.activation(bonus[h], lean[h], ACT.Copy, scale=lam_col[:])
         nc.scalar.activation(own[1], a[:].indirect(half_of(own_list, 1)), ACT.Copy)
+        f2 = sb.tile([P, T], F32, name="f2", tag="row")
+        nc.gpsimd.memset(f2[:], 0.0)
         for h in range(2):
-            nc.vector.tensor_tensor(f1[:].indirect(half_of(own_list, h)), own[h], bonus[h], ALU.add)
-        nc.vector.tensor_tensor(f2[:].indirect(put_list[:]), own_all[:], bonus_all[:], ALU.add)
+            nc.vector.tensor_tensor(f1[h][:].indirect(half_of(own_list, h)), own[h], bonus[h], ALU.add)
+        nc.vector.tensor_tensor(f2[:].indirect(put_list[:]), own_all, bonus_all[:], ALU.add)
 
         blocks = BANK // P
         turned = [ps.tile([P, BANK], F32, name="turned%d" % b) for b in range(T // BANK)]
-        for b in range(T // BANK):
-            for j in range(blocks):
-                nc.tensor.matmul(
-                    turned[b][:, j * P : (j + 1) * P],
-                    old_sb[:, b * BANK + j * P : b * BANK + (j + 1) * P],
-                    ident[:],
-                    start=(j == 0),
-                    stop=False,
-                    is_transpose=True,
-                )
+        terms = [old_sb, f1a, f1b]
+        for i, term in enumerate(terms):
+            for b in range(T // BANK):
+                for j in range(blocks):
+                    nc.tensor.matmul(
+                        turned[b][:, j * P : (j + 1) * P],
+                        term[:, b * BANK + j * P : b * BANK + (j + 1) * P],
+                        ident[:],
+                        start=(i == 0 and j == 0),
+                        stop=(i == len(terms) - 1 and j == blocks - 1),
+                        is_transpose=True,
+                    )
         base = []
-        for b in range(T // BANK):
-            for j in range(blocks):
-                nc.tensor.matmul(
-                    turned[b][:, j * P : (j + 1) * P],
-                    f1[:, b * BANK + j * P : b * BANK + (j + 1) * P],
-                    ident[:],
-                    start=False,
-                    stop=(j == blocks - 1),
-                    is_transpose=True,
-                )
         for b in range(T // BANK):
             turned_sb = sb.tile([P, BANK], F32, name="turned_sb%d" % b)
             nc.scalar.copy(out=turned_sb[:], in_=turned[b][:])
-            back = ps.tile([P, BANK], F32, name="back%d" % b)
+            back = ps.tile([P, BANK], F32, name="back%d" % b, tag="bank%d" % b)
             for j in range(blocks):
                 nc.tensor.transpose(back[:, j * P : (j + 1) * P], turned_sb[:, j * P : (j + 1) * P], ident[:])
             base.append(back)

@@ -31,6 +31,7 @@ def tile_attend_seconded_lean_twiceput_heads_kernel(
     nc = tc.nc
     with ExitStack() as ctx:
         lists = ctx.enter_context(tc.tile_pool(name="lists", bufs=1))
+        reuse = ctx.enter_context(tc.tile_pool(name="reuse", bufs=1))
         sb = ctx.enter_context(tc.tile_pool(name="sb", bufs=1))
         ps = ctx.enter_context(tc.psum_pool(name="ps", bufs=1))
 
@@ -40,10 +41,10 @@ def tile_attend_seconded_lean_twiceput_heads_kernel(
         nc.sync.dma_start(out=k_words[:].bitcast(I32), in_=keys_words[0].bitcast(I32))
         k_scales = sb.tile([P, T], U8, name="k_scales", align_bytes=64)
         nc.vector.memset(k_scales[:].bitcast(U32), 0)
-        for quad in range(4):
+        for r in range(4):
             nc.sync.dma_start(
-                out=k_scales[32 * quad : 32 * quad + 4, :].bitcast(I32),
-                in_=keys_scales[0, 4 * quad : 4 * quad + 4, :].bitcast(I32),
+                out=k_scales[r:P:32, :].bitcast(I32),
+                in_=keys_scales[0, r:16:4, :].bitcast(I32),
             )
 
         def load_list(src, name):
@@ -54,18 +55,18 @@ def tile_attend_seconded_lean_twiceput_heads_kernel(
         opp_list = load_list(offs3, "opp_list")
         sec_list = load_list(offs2, "sec_list")
         own_list = load_list(offs, "own_list")
-        lam_col = sb.tile([P, 1], F32, name="lam_col")
-        nc.gpsimd.dma_start(out=lam_col[:], in_=lam)
-        share_col = sb.tile([P, 1], F32, name="share_col")
-        nc.gpsimd.dma_start(out=share_col[:], in_=share2)
         put_list = load_list(offs4, "put_list")
+        lam_col = sb.tile([P, 1], F32, name="lam_col")
+        nc.sync.dma_start(out=lam_col[:], in_=lam)
+        share_col = sb.tile([P, 1], F32, name="share_col")
+        nc.sync.dma_start(out=share_col[:], in_=share2)
 
-        ident = sb.tile([P, P], F32, name="ident")
-        make_identity(nc, ident[:])
         f1a = sb.tile([P, T], F32, name="f1a")
         nc.vector.memset(f1a[:], 0.0)
+        f2 = sb.tile([P, T], F32, name="f2")
+        nc.vector.memset(f2[:], 0.0)
 
-        q_bf = sb.tile([P, Q, PACK], BF16, name="q_bf", tag="first", align_bytes=64)
+        q_bf = reuse.tile([P, Q, PACK], BF16, name="q_bf", offset=0, align_bytes=64)
         nc.vector.tensor_copy(
             out=q_bf[:].rearrange("p (c i) t -> p c t i", i=4),
             in_=q_raw[:].rearrange("p t (c i) -> p c t i", i=4),
@@ -78,10 +79,12 @@ def tile_attend_seconded_lean_twiceput_heads_kernel(
             out=q_codes[:].bitcast(FP8X4), scales=q_scales[:], in_=q_bf[:].rearrange("p q t -> p (q t)")
         )
 
-        f1b = sb.tile([P, T], F32, name="f1b", tag="first", align_bytes=64)
-        nc.gpsimd.memset(f1b[:], 0.0)
+        ident = reuse.tile([P, P], F32, name="ident", offset=0)
+        make_identity(nc, ident[:])
+        f1b = reuse.tile([P, T], F32, name="f1b", offset=4 * P)
+        nc.vector.memset(f1b[:], 0.0)
         f1 = [f1a, f1b]
-        a = sb.tile([P, T], F32, name="a", tag="row")
+        a = sb.tile([P, T], F32, name="a")
         for n, width in enumerate(MM_PIECES):
             cols = slice(sum(MM_PIECES[:n]), sum(MM_PIECES[: n + 1]))
             acc = ps.tile([P, width], F32, name="acc%d" % n, tag="bank%d" % n)
@@ -123,8 +126,6 @@ def tile_attend_seconded_lean_twiceput_heads_kernel(
             nc.scalar.activation(lean[h], diff[h][:], ACT.Tanh)
             nc.scalar.activation(bonus[h], lean[h], ACT.Copy, scale=lam_col[:])
         nc.scalar.activation(own[1], a[:].indirect(half_of(own_list, 1)), ACT.Copy)
-        f2 = sb.tile([P, T], F32, name="f2", tag="row")
-        nc.gpsimd.memset(f2[:], 0.0)
         for h in range(2):
             nc.vector.tensor_tensor(f1[h][:].indirect(half_of(own_list, h)), own[h], bonus[h], ALU.add)
         nc.vector.tensor_tensor(f2[:].indirect(put_list[:]), own_all, bonus_all[:], ALU.add)

@@ -21,6 +21,8 @@ P = 128
 PACK = 4
 MM_PIECES = (256, 256, 256, 128, 128)
 HALF = SLOTS // 2
+QUARTER = SLOTS // 4
+CAST_SPLIT = 88
 BANK = 512
 OUT_PIECES = (256, 256, 256, 128, 128)
 
@@ -31,7 +33,6 @@ def tile_attend_seconded_lean_twiceput_heads_kernel(
     nc = tc.nc
     with ExitStack() as ctx:
         lists = ctx.enter_context(tc.tile_pool(name="lists", bufs=1))
-        reuse = ctx.enter_context(tc.tile_pool(name="reuse", bufs=1))
         sb = ctx.enter_context(tc.tile_pool(name="sb", bufs=1))
         ps = ctx.enter_context(tc.psum_pool(name="ps", bufs=1))
 
@@ -61,16 +62,19 @@ def tile_attend_seconded_lean_twiceput_heads_kernel(
         share_col = sb.tile([P, 1], F32, name="share_col")
         nc.sync.dma_start(out=share_col[:], in_=share2)
 
+        ident = sb.tile([P, P], F32, name="ident")
+        make_identity(nc, ident[:])
         f1a = sb.tile([P, T], F32, name="f1a")
         nc.vector.memset(f1a[:], 0.0)
         f2 = sb.tile([P, T], F32, name="f2")
         nc.vector.memset(f2[:], 0.0)
 
-        q_bf = reuse.tile([P, Q, PACK], BF16, name="q_bf", offset=0, align_bytes=64)
-        nc.vector.tensor_copy(
-            out=q_bf[:].rearrange("p (c i) t -> p c t i", i=4),
-            in_=q_raw[:].rearrange("p t (c i) -> p c t i", i=4),
-        )
+        q_bf = sb.tile([P, Q, PACK], BF16, name="q_bf", tag="first", align_bytes=64)
+        for copy, cols in ((nc.vector.tensor_copy, slice(0, CAST_SPLIT)), (nc.scalar.copy, slice(CAST_SPLIT, Q))):
+            copy(
+                out=q_bf[:, cols, :].rearrange("p (c i) t -> p c t i", i=4),
+                in_=q_raw[:, :, cols].rearrange("p t (c i) -> p c t i", i=4),
+            )
         old_sb = sb.tile([P, T], F32, name="old_sb", tag="load")
         nc.sync.dma_start(out=old_sb[:], in_=old)
         q_codes = sb.tile([P, Q], U32, name="q_codes", align_bytes=64)
@@ -79,10 +83,8 @@ def tile_attend_seconded_lean_twiceput_heads_kernel(
             out=q_codes[:].bitcast(FP8X4), scales=q_scales[:], in_=q_bf[:].rearrange("p q t -> p (q t)")
         )
 
-        ident = reuse.tile([P, P], F32, name="ident", offset=0)
-        make_identity(nc, ident[:])
-        f1b = reuse.tile([P, T], F32, name="f1b", offset=4 * P)
-        nc.vector.memset(f1b[:], 0.0)
+        f1b = sb.tile([P, T], F32, name="f1b", tag="first", align_bytes=64)
+        nc.gpsimd.memset(f1b[:], 0.0)
         f1 = [f1a, f1b]
         a = sb.tile([P, T], F32, name="a")
         for n, width in enumerate(MM_PIECES):
@@ -115,16 +117,22 @@ def tile_attend_seconded_lean_twiceput_heads_kernel(
         own = [own_all[:, h * HALF : (h + 1) * HALF] for h in range(2)]
         bonus = [bonus_all[:, h * HALF : (h + 1) * HALF] for h in range(2)]
         lean = [strip[:, 3 * HALF // 2 : 5 * HALF // 2], strip[:, 2 * HALF : 3 * HALF]]
-        sec0 = own[0]
+        sec0_tile = sb.tile([P, HALF], F32, name="sec0")
+        sec0 = sec0_tile[:]
         nc.scalar.activation(opp[0][:], a[:].indirect(half_of(opp_list, 0)), ACT.Copy)
         nc.vector.tensor_copy(sec0, a[:].indirect(half_of(sec_list, 0)))
         nc.scalar.activation(opp[1][:], a[:].indirect(half_of(opp_list, 1)), ACT.Copy)
-        nc.vector.tensor_tensor(diff[0][:], sec0, opp[0][:], ALU.subtract)
+        quarters = [slice(0, QUARTER), slice(QUARTER, HALF)]
+        for cols in quarters:
+            nc.vector.tensor_tensor(diff[0][:, cols], sec0[:, cols], opp[0][:, cols], ALU.subtract)
         nc.vector.tensor_copy(own[0], a[:].indirect(half_of(own_list, 0)))
         nc.vector.tensor_tensor(diff[1][:], a[:].indirect(half_of(sec_list, 1)), opp[1][:], ALU.subtract)
-        for h in range(2):
-            nc.scalar.activation(lean[h], diff[h][:], ACT.Tanh)
-            nc.scalar.activation(bonus[h], lean[h], ACT.Copy, scale=lam_col[:])
+        for cols in quarters:
+            nc.scalar.activation(lean[0][:, cols], diff[0][:, cols], ACT.Tanh)
+        for cols in quarters:
+            nc.scalar.activation(bonus[0][:, cols], lean[0][:, cols], ACT.Copy, scale=lam_col[:])
+        nc.scalar.activation(lean[1], diff[1][:], ACT.Tanh)
+        nc.scalar.activation(bonus[1], lean[1], ACT.Copy, scale=lam_col[:])
         nc.scalar.activation(own[1], a[:].indirect(half_of(own_list, 1)), ACT.Copy)
         for h in range(2):
             nc.vector.tensor_tensor(f1[h][:].indirect(half_of(own_list, h)), own[h], bonus[h], ALU.add)

from contextlib import ExitStack

import concourse.mybir as mybir
from concourse.masks import make_identity

D, T, SLOTS, Q = 512, 1024, 512, 128
FLOPS = 2 * D * T * Q

F32 = mybir.dt.float32
BF16 = mybir.dt.bfloat16
I32 = mybir.dt.int32
U32 = mybir.dt.uint32
U16 = mybir.dt.uint16
U8 = mybir.dt.uint8
FP8X4 = mybir.dt.float8_e4m3fn_x4
FP4X4 = mybir.dt.float4_e2m1fn_x4
ALU = mybir.AluOpType
ACT = mybir.ActivationFunctionType

P = 128
PACK = 4
MM_PIECES = (256, 256, 256, 128, 128)
HALF = SLOTS // 2
QUARTER = SLOTS // 4
CAST_SPLIT = 88
BANK = 512
OUT_PIECES = (256, 256, 256, 128, 128)


def tile_attend_seconded_lean_twiceput_heads_kernel(
    tc, query, keys_words, keys_scales, lam, old, share2, offs, offs2, offs3, offs4, out
):
    nc = tc.nc
    with ExitStack() as ctx:
        lists = ctx.enter_context(tc.tile_pool(name="lists", bufs=1))
        sb = ctx.enter_context(tc.tile_pool(name="sb", bufs=1))
        ps = ctx.enter_context(tc.psum_pool(name="ps", bufs=1))

        q_raw = sb.tile([P, PACK, Q], F32, name="q_raw", tag="load")
        nc.sync.dma_start(out=q_raw[:], in_=query.rearrange("(p j) q -> p j q", j=PACK))
        k_words = sb.tile([P, 2 * T], U8, name="k_words", align_bytes=64)
        nc.sync.dma_start(out=k_words[:].bitcast(I32), in_=keys_words[0].bitcast(I32))
        k_scales = sb.tile([P, T], U8, name="k_scales", align_bytes=64)
        nc.vector.memset(k_scales[:].bitcast(U32), 0)
        for r in range(4):
            nc.sync.dma_start(
                out=k_scales[r:P:32, :].bitcast(I32),
                in_=keys_scales[0, r:16:4, :].bitcast(I32),
            )

        def load_list(src, name):
            tile = lists.tile([P, SLOTS // 16], U16, name=name)
            nc.sync.dma_start(tile[:], src)
            return tile

        opp_list = load_list(offs3, "opp_list")
        sec_list = load_list(offs2, "sec_list")
        own_list = load_list(offs, "own_list")
        put_list = load_list(offs4, "put_list")
        lam_col = sb.tile([P, 1], F32, name="lam_col")
        nc.sync.dma_start(out=lam_col[:], in_=lam)
        share_col = sb.tile([P, 1], F32, name="share_col")
        nc.sync.dma_start(out=share_col[:], in_=share2)

        ident = sb.tile([P, P], F32, name="ident")
        make_identity(nc, ident[:])
        f1a = sb.tile([P, T], F32, name="f1a")
        nc.vector.memset(f1a[:], 0.0)
        f2 = sb.tile([P, T], F32, name="f2")
        nc.vector.memset(f2[:], 0.0)

        q_bf = sb.tile([P, Q, PACK], BF16, name="q_bf", tag="first", align_bytes=64)
        for copy, cols in ((nc.vector.tensor_copy, slice(0, CAST_SPLIT)), (nc.scalar.copy, slice(CAST_SPLIT, Q))):
            copy(
                out=q_bf[:, cols, :].rearrange("p (c i) t -> p c t i", i=4),
                in_=q_raw[:, :, cols].rearrange("p t (c i) -> p c t i", i=4),
            )
        old_sb = sb.tile([P, T], F32, name="old_sb", tag="load")
        nc.sync.dma_start(out=old_sb[:], in_=old)
        q_codes = sb.tile([P, Q], U32, name="q_codes", align_bytes=64)
        q_scales = sb.tile([P, Q], U8, name="q_scales", align_bytes=64)
        nc.vector.quantize_mx(
            out=q_codes[:].bitcast(FP8X4), scales=q_scales[:], in_=q_bf[:].rearrange("p q t -> p (q t)")
        )

        f1b = sb.tile([P, T], F32, name="f1b", tag="first", align_bytes=64)
        nc.gpsimd.memset(f1b[:], 0.0)
        f1 = [f1a, f1b]
        a = sb.tile([P, T], F32, name="a")
        for n, width in enumerate(MM_PIECES):
            cols = slice(sum(MM_PIECES[:n]), sum(MM_PIECES[: n + 1]))
            acc = ps.tile([P, width], F32, name="acc%d" % n, tag="bank%d" % n)
            nc.tensor.matmul_mx(
                out=acc[:],
                lhsT=q_codes[:].bitcast(FP8X4),
                lhsT_scale=q_scales[:],
                rhs=k_words[:, 2 * cols.start : 2 * cols.stop].bitcast(FP4X4),
                rhs_scale=k_scales[:, cols],
                start=True,
                stop=True,
            )
            if n % 2 == 1:
                nc.scalar.copy(out=a[:, cols], in_=acc[:])
            else:
                nc.vector.tensor_copy(out=a[:, cols], in_=acc[:])

        def half_of(tile, h):
            return tile[:, h * HALF // 16 : (h + 1) * HALF // 16]

        def halves(name):
            return [sb.tile([P, HALF], F32, name="%s%d" % (name, h)) for h in range(2)]

        opp, diff = halves("opp"), halves("diff")
        strip = sb.tile([P, 3 * HALF], F32, name="strip")
        own_all = strip[:, 0:SLOTS]
        bonus_all = sb.tile([P, SLOTS], F32, name="bonus_all")
        own = [own_all[:, h * HALF : (h + 1) * HALF] for h in range(2)]
        bonus = [bonus_all[:, h * HALF : (h + 1) * HALF] for h in range(2)]
        lean = [strip[:, 3 * HALF // 2 : 5 * HALF // 2], strip[:, 2 * HALF : 3 * HALF]]
        sec0_tile = sb.tile([P, HALF], F32, name="sec0")
        sec0 = sec0_tile[:]
        nc.scalar.activation(opp[0][:], a[:].indirect(half_of(opp_list, 0)), ACT.Copy)
        nc.vector.tensor_copy(sec0, a[:].indirect(half_of(sec_list, 0)))
        nc.scalar.activation(opp[1][:], a[:].indirect(half_of(opp_list, 1)), ACT.Copy)
        quarters = [slice(0, QUARTER), slice(QUARTER, HALF)]
        for cols in quarters:
            nc.vector.tensor_tensor(diff[0][:, cols], sec0[:, cols], opp[0][:, cols], ALU.subtract)
        nc.vector.tensor_copy(own[0], a[:].indirect(half_of(own_list, 0)))
        nc.vector.tensor_tensor(diff[1][:], a[:].indirect(half_of(sec_list, 1)), opp[1][:], ALU.subtract)
        for cols in quarters:
            nc.scalar.activation(lean[0][:, cols], diff[0][:, cols], ACT.Tanh)
        for cols in quarters:
            nc.scalar.activation(bonus[0][:, cols], lean[0][:, cols], ACT.Copy, scale=lam_col[:])
        nc.scalar.activation(lean[1], diff[1][:], ACT.Tanh)
        nc.scalar.activation(bonus[1], lean[1], ACT.Copy, scale=lam_col[:])
        nc.scalar.activation(own[1], a[:].indirect(half_of(own_list, 1)), ACT.Copy)
        for h in range(2):
            nc.vector.tensor_tensor(f1[h][:].indirect(half_of(own_list, h)), own[h], bonus[h], ALU.add)
        nc.vector.tensor_tensor(f2[:].indirect(put_list[:]), own_all, bonus_all[:], ALU.add)

        blocks = BANK // P
        turned = [ps.tile([P, BANK], F32, name="turned%d" % b) for b in range(T // BANK)]
        terms = [old_sb, f1a, f1b]
        for i, term in enumerate(terms):
            for b in range(T // BANK):
                for j in range(blocks):
                    nc.tensor.matmul(
                        turned[b][:, j * P : (j + 1) * P],
                        term[:, b * BANK + j * P : b * BANK + (j + 1) * P],
                        ident[:],
                        start=(i == 0 and j == 0),
                        stop=(i == len(terms) - 1 and j == blocks - 1),
                        is_transpose=True,
                    )
        base = []
        for b in range(T // BANK):
            turned_sb = sb.tile([P, BANK], F32, name="turned_sb%d" % b)
            nc.scalar.copy(out=turned_sb[:], in_=turned[b][:])
            back = ps.tile([P, BANK], F32, name="back%d" % b, tag="bank%d" % b)
            for j in range(blocks):
                nc.tensor.transpose(back[:, j * P : (j + 1) * P], turned_sb[:, j * P : (j + 1) * P], ident[:])
            base.append(back)

        start = 0
        for i, width in enumerate(OUT_PIECES):
            piece = sb.tile([P, width], F32, name="piece%d" % i)
            b, off = divmod(start, BANK)
            nc.vector.scalar_tensor_tensor(
                out=piece[:],
                in0=f2[:, start : start + width],
                scalar=share_col[:],
                in1=base[b][:, off : off + width],
                op0=ALU.mult,
                op1=ALU.add,
            )
            queue = nc.sync if i % 2 == 0 else nc.scalar
            queue.dma_start(out=out[:, start : start + width], in_=piece[:])
            start = start + width
